import numpy as np, ml_dtypes
CORES = [66,74,82,90,194,202,210,218]
N = 8
BF = ml_dtypes.bfloat16
W, K, P, RO, LIM = 4096, 8, 256, 6, 88
def hashed(u, v):
    u = u & 4095; v = v & 4095
    return ((u * v >> 5) + 37 * u) & (W - 1)
def probe(w, v):
    s = np.matmul(w, v.astype(np.float32)).astype(np.int64)
    return hashed(s[:, :, 0], s[:, :, 1])
def masks(rng, size):
    o = np.argsort(np.argsort(rng.random((N, 8, 16, K)), axis=2), axis=2)
    return (o < size[:, :, None, :]).astype(np.int32)
def parts(rng):
    x = rng.integers(0, 256, (N, 8, 16, W), dtype=np.uint8).astype(np.int32)
    return x, masks(rng, rng.integers(4, 12, (N, 8, K))), rng.integers(0, 256, (N, 8, 16, P)), rng.integers(0, 256, (N, 8, 16, 2))
def pack(x, m, z, w):
    return {a: np.ascontiguousarray(v.reshape(N, 128, n)).astype(np.float32).astype(BF) for a, v, n in (("xr", x, W), ("m0", m, K), ("z0", z, P), ("wt", w, 2))}
def setup_inputs(rng):
    return pack(*parts(rng))
def setup_inputs_spread(rng):
    def uneven(n):
        v = (np.exp2(8 * rng.random((N, 8, 1, n))) * rng.random((N, 8, 16, n))).astype(np.int32)
        return np.where(rng.random((N, 8, 1, n)) < 0.5, v, 255 - v)
    lo = rng.choice(np.array([0, 2, 5]), (N, 8, 1))
    return pack(uneven(W), masks(rng, lo + ((17 - lo) * rng.random((N, 8, K))).astype(np.int64)), uneven(P), np.exp2(8 * rng.random((N, 8, 16, 2))).astype(np.int64))
def setup_inputs_ends(rng):
    def two(n): return 255 * rng.integers(0, 2, (N, 8, 16, n), dtype=np.int32)
    x, z, w = two(W), two(P), two(2); m = rng.integers(0, 2, (N, 8, 16, K))
    s = 255 * rng.integers(0, 2, (8, 8, 1)); s[7] = 255
    z[N - 1, :, :8] = s; x[N - 1, :, :8] = 255 - s
    z[1, 7, :8] = 255; x[1, 7, :8] = 0
    for q, g in [(N - 1, g) for g in range(8)] + [(1, 7)]:
        a = rng.integers(0, 8, K); b = (a + rng.integers(1, 8, K)) % 8
        m[q, g, a, np.arange(K)] = 1; m[q, g, b, np.arange(K)] = 1
    m[1, 7, :, K - 1] = 0; m[1, 7, 15, K - 1] = 1
    w[N - 1, 7] = 255; m[N - 1, 7, :, 0] = 1; m[N - 1, 7, :, K - 1] = 1
    for i in (0, 1, 6, P - 1): z[N - 1, 7, :, i] = 255
    x[N - 1, 7, :, int(hashed(16 * 255 * 255, 16 * 255 * 255))] = 0
    for i in (0, 3, P - 1): z[0, 7, :, i] = 0
    x[0, 7, :, 0] = 0; m[0, 6, :, K - 1] = 0
    for g, e in ((7, 0), (5, 1)):
        w[2, g, :, e] = 255; w[2, g, :, 1 - e] = 255 * (rng.permutation(16) < rng.integers(1, 16))
        m[2, g, :, 0] = 1; x[2, g, 0] = 0
        for i in (0, 3, P - 1): z[2, g, :, i] = 255
        x[2, g, :, int(hashed(255 * int(np.sum(w[2, g, :, 0])), 255 * int(np.sum(w[2, g, :, 1]))))] = 255
    x[2, 6, 14:16] = 0; z[2, 6, 14:16, :8] = 255
    m[2, 6, :, 0] = 0; m[2, 6, 14] = 0; m[2, 6, 14:16, 0] = 1
    return pack(x, m, z, w)
def setup_inputs_corners(rng):
    x, m, z, w = parts(rng); idx = np.concatenate([np.arange(0, P, 2), np.array([P - 1])])
    t = np.argwhere(hashed(np.arange(256)[:, None], np.arange(256)[None, :]) == W - 1)
    for q in range(N):
        order = rng.permutation(8)
        want = {0: 0, 1: 7, N - 2: 0, N - 1: 4}.get(q)
        if want is not None:
            i = int(np.argmax(order == want)); order[i] = order[7]; order[7] = want
        for g in range(8):
            a, b, c, e = x[q, g], m[q, g], z[q, g], w[q, g]; kind = int(order[g])
            if kind == 0: b[:, 0] = 0
            if kind == 1: b[:] = 1
            if kind == 2:
                b[:] = 1; b[:, K - 1] = 0; b[15, K - 1] = 1
            if kind == 3:
                a[:] = rng.integers(250, 256, a.shape); c[:] = rng.integers(0, 6, c.shape)
                b[:] = np.argsort(np.argsort(rng.random((16, K)), axis=0), axis=0) < rng.integers(2, 4, (1, K))
            if kind == 4:
                e[:] = 0; e[0, 0] = 1; e[1, 1] = 1; b[0:2] = 1
                p = t[rng.integers(0, len(t), len(idx))]; c[0, idx] = p[:, 0]; c[1, idx] = p[:, 1]; c[0, 1] = 0
            if kind == 5:
                e[:] = 0; e[0] = 15; e[1] = 27; b[0:2] = 1; c[0, idx] = 255; c[1, idx] = 10
            if kind == 6:
                a[:] = 128; c[:] = 128 + rng.choice(np.array([-LIM - 1, -LIM, LIM, LIM + 1]), c.shape)
    p = t[rng.integers(0, len(t))]; odd = np.arange(2 * int(rng.integers(0, P // 4)) + 1, P, 2)
    m[N - 1, 7, :, 0] = 0; m[N - 1, 7, 0:2, 0] = 1; x[N - 1, 7, 0:2, W - 1] = p
    z[N - 1, 7, 0] = 0; z[N - 1, 7, 0, odd] = p[0]; z[N - 1, 7, 1, odd] = p[1]
    z[N - 2, 7, 0] = p[0]; z[N - 2, 7, 1] = p[1]; x[N - 2, 7, :, 0] = 0
    o = rng.permutation(256)[:P]
    w[1, 7] = 0; w[1, 7, 0, 0] = 1; m[1, 7, :, 0] = 0; m[1, 7, 0, 0] = 1; z[1, 7, 0] = o
    z[0, 7, 0] = o[P - 1]; x[0, 7, :, 0] = 0
    return pack(x, m, z, w)
def setup_inputs_crowd(rng):
    x, m, z, w = parts(rng); role = rng.permutation(N)
    for q in range(N):
        r = int(role[q]); k = rng.permutation(8)
        if r == 1: k = np.roll(k, 4 - int(np.argmax(k == rng.integers(3, 5))))
        if r < 3: x[q] = rng.integers(200, 256, (8, 16, W))
        if r < 2: z[q] = rng.integers(0, 101, (8, 16, P))
        if r == 2: z[q] = rng.integers(200, 256, (8, 16, P))
        w[q, k[0]] = 0; w[q, k[1]] = 0
        for g in k[2:4]:
            w[q, g] = 0; w[q, g, 0] = 1; m[q, g, 0] = 1
            c = int(rng.integers(0, 100)) if r < 2 else int(rng.integers(200, 255))
            z[q, g, 0] = c; z[q, g, 0, int(rng.integers(0, P))] = c + 1
        if r == 1: z[q, k[4], :, int(rng.integers(0, P))] = 210
        if r == 2: z[q, k[4], :, int(rng.integers(0, P))] = 50
    return pack(x, m, z, w)
def check_inputs(d):
    bad = []
    for k, lo, hi in (("xr", 0, 255), ("m0", 0, 1), ("z0", 0, 255), ("wt", 0, 255)):
        a = np.asarray(d[k]).astype(np.float32)
        if not (np.min(a) >= lo and np.max(a) <= hi): bad.append("range of " + k)
        elif np.any(a != np.floor(a)): bad.append("whole numbers in " + k)
    return bad
def reference(xr, m0, z0, wt):
    X = xr.astype(np.float32).astype(np.int16).reshape(N, 8, 16, W)
    M = np.repeat(m0.astype(np.float32).astype(np.int16).reshape(N, 8, 16, K)[..., None], P, axis=4)
    z = z0.astype(np.float32).astype(np.int16).reshape(N, 8, 16, P)
    w = np.ascontiguousarray(wt.astype(np.float32).reshape(N, 8, 16, 2).transpose(0, 1, 3, 2))
    A = np.zeros(N, np.int64); kk = np.arange(K)[None, None, :, None]; steps = []
    for t in range(RO):
        zk = z[:, :, :, None, :]
        h = probe(w, (M * zk).reshape(N, 8, 16, K * P))
        Xh = np.take_along_axis(X, h[:, :, None, :], 3).reshape(N, 8, 16, K, P)
        F = M * (np.abs(Xh - zk) > LIM)
        ok = np.add.reduce(F, axis=2, dtype=np.int16) <= (1 + (A & 1))[:, None, None, None]
        j = np.where(np.any(ok, axis=2), np.argmax(ok, axis=2), K)
        first = F * (np.add.accumulate(F, axis=2, dtype=np.int16) == 1)
        U = np.max(first * (kk < j[:, :, None, :])[:, :, None], axis=3)
        hit = (j < K)[:, :, None, :]; s = np.where(j < K, j, 0)[:, :, None, None, :]
        U = np.maximum(U, hit * np.take_along_axis(M, s, 3)[:, :, :, 0])
        xs = np.take_along_axis(Xh, s, 3)[:, :, :, 0]
        new = np.where(hit, np.abs(z - xs), (z + xs) >> 1)
        down = (kk[:, :, 1:] <= j[:, :, None, :])[:, :, None]
        M = np.concatenate([U[:, :, :, None], np.where(down, M[:, :, :, :-1], M[:, :, :, 1:])], axis=3)
        if t < RO - 1:
            place = probe(w, U * z)
            for q in range(N):
                for g in range(8):
                    v, i = np.unique(place[q, g], return_index=True)
                    X[q, g][:, v] = z[q, g][:, i]
        A = np.add.reduce((j == K).astype(np.int64), axis=(1, 2))
        steps.append(new); z = np.roll(new, 1, axis=0)
    return {"ym": M.reshape(N, 128, K * P).astype(np.float32).astype(BF), "yz": np.stack(steps, axis=3).reshape(N, 128, RO * P).astype(np.float32).astype(BF)}

from concourse.mybir import dt, AluOpType, AxisListType, ActivationFunctionType

A = AluOpType
FN = ActivationFunctionType
STEPS, NP, NK, NW, LIMIT = 6, 256, 8, 4096, 88
MAGIC = 12582912.0
B16, F32, I32, U16, F16 = "bfloat16", "float32", "int32", "uint16", "float16"
MZV, MZS = (0, 1), (2, 3)
SB = {0: 7, 2: 5}
NOB = 3
NSC = 5

_SB = {
    "tab": (NW + 16, B16), "mska": (2304, B16), "mskb": (2304, B16), "mz": (2048, B16), "yy": (2048, B16), "xh": (2048, B16),
    "ab": (2048, B16), "ff": (2048, B16), "fr": (2048, B16), "mini": (8, B16), "wts": (2, B16), "ones": (512, B16),
    "ident": (128, B16), "nident": (128, B16), "ident256": (128, B16), "idm512": (128, B16), "id600": (128, B16),
    "idpow": (1024, B16), "triw": (128, B16), "sel": (144, B16), "bigu": (144, B16), "bigv": (144, B16),
    "shf": (1920, B16), "shh": (1920, F16), "cmpt": (240, F32), "k4": (128, F32), "baseoff": (128, F32),
    "qi": (8, I32), "qf": (8, F32), "dum": (8, F32), "m256": (8, F32), "sgn": (16, B16), "ctab": (8, F32), "thrt": (16, B16),
    "hi0": (128, I32), "hi1": (128, I32), "hi2": (32, I32), "ha0": (64, I32), "ha1": (64, I32), "ha2": (16, I32),
    "hb0": (64, I32), "hb1": (64, I32), "hb2": (16, I32), "hu0": (64, U16), "hu1": (64, U16), "bs0": (64, F32), "bs1": (64, F32),
    "nk0": (64, F32), "nk1": (64, F32), "ky0": (64, F32), "ky1": (64, F32), "ka0": (32, F32), "ka1": (32, F32),
    "kb0": (16, F32), "kb1": (16, F32), "key": (16, I32), "hs": (16, I32), "hsu": (16, U16), "nmu": (16, U16), "nmf": (16, B16),
    "jr": (16, I32), "jru": (16, U16), "ob": (128, F32), "of": (128, F32), "offu": (128, U16),
    "sz": (256, B16), "yh": (256, F32), "cc": (256, F32), "wh": (256, F32), "thr": (256, B16), "u1": (256, B16), "uz": (256, B16),
    "asum": (1, F32), "ai": (8, I32), "lim": (8, F32), "pl": (16, I32), "hlb": (16, F16), "eq": (240, B16),
    "lo": (16, F32), "so": (16, F32), "scu": (32, U16),
}
SCRATCH = {}
for _n in _SB:
    SCRATCH[_n] = ("sbuf", [128, _SB[_n][0]], _SB[_n][1])
for _t in range(STEPS):
    SCRATCH["zin%d" % _t] = ("sbuf", [128, NP], B16)
    SCRATCH["nz%d" % _t] = ("sbuf", [128, NP], B16)
for _b in range(8):
    SCRATCH["ps%d" % _b] = ("psum", [128, 512], F32)

SEMAPHORES = ["sv", "ss", "sp", "sg", "sent", "ldw", "ldm", "ldz", "ldx", "outs"] + ["arr%d" % t for t in range(1, STEPS)]


def rank_program(g, core, T, topo):
    rank = T.rank_of(core)
    if rank is None:
        return
    nxt_core = T.cores[(rank + 1) % len(T.cores)]
    prv_core = T.cores[(rank - 1) % len(T.cores)]
    V, S, P = g.vector, g.scalar, g.tensor

    semof = {"V": "sv", "S": "ss", "P": "sp", "G": "sg"}
    waiter = {"V": V.wait_ge, "S": S.wait_ge, "P": P.wait_ge, "G": g.wait_ge, "Y": g.sync.wait_ge}
    count = {"V": 0, "S": 0, "P": 0, "G": 0}
    known = {"V": {}, "S": {}, "P": {}, "G": {}, "Y": {}}
    snap, lastw, readers, bankuse = {}, {}, {}, {}

    def hold(e, r, w, banks):
        deps = {}

        def dep(f, n):
            if known[e].get(f, 0) < n and deps.get(f, 0) < n:
                deps[f] = n
        for tag in r:
            if tag in lastw:
                dep(*lastw[tag])
        for tag in w:
            if tag in lastw and (lastw[tag][0] != e or tag == "tab"):
                dep(*lastw[tag])
            for f, n in readers.get(tag, {}).items():
                if f != e:
                    dep(f, n)
        for b in banks:
            for f, n in bankuse.get(b, {}).items():
                if f != e:
                    dep(f, n)
        for f in sorted(deps):
            n = deps[f]
            if any(f2 != f and snap.get((f2, n2), {}).get(f, 0) >= n for f2, n2 in deps.items()):
                continue
            waiter[e](T.sem[semof.get(f, f)], n)
        for f, n in deps.items():
            for f2, n2 in snap.get((f, n), {}).items():
                if known[e].get(f2, 0) < n2:
                    known[e][f2] = n2
            known[e][f] = max(known[e].get(f, 0), n)

    def note(f, n, r, w, banks):
        for tag in w:
            lastw[tag] = (f, n)
            readers[tag] = {}
        for tag in r:
            readers.setdefault(tag, {})[f] = n
        for b in banks:
            bankuse.setdefault(b, {})[f] = n

    def op(e, call, r, w, banks=(), **kw):
        hold(e, r, w, banks)
        count[e] += 1
        n = count[e]
        call(**kw).then_inc(T.sem[semof[e]], 1)
        snap[(e, n)] = dict(known[e])
        note(e, n, r, w, banks)

    def dma(e, call, sem, val, r, w, **kw):
        hold(e, r, w, ())
        call(**kw).then_inc(T.sem[sem], 16)
        note(sem, val, r, w, ())

    def tt(out, in0, in1, o, r, w, banks=()):
        op("V", V.tensor_tensor, r, w, banks, out=out, in0=in0, in1=in1, op=o)

    def ts(out, in0, s1, o1, r, w, banks=(), s2=None, o2=None):
        if o2 is None:
            op("V", V.tensor_scalar, r, w, banks, out=out, in0=in0, scalar1=s1, scalar2=None, op0=o1)
        else:
            op("V", V.tensor_scalar, r, w, banks, out=out, in0=in0, scalar1=s1, scalar2=s2, op0=o1, op1=o2)

    def cp(out, in_, r, w, banks=()):
        op("V", V.tensor_copy, r, w, banks, out=out, in_=in_)

    def act(out, in_, func, r, w, banks=(), **kw):
        op("S", S.activation, r, w, banks, out=out, in_=in_, func=func, **kw)

    def mm(b, c0, c1, lhsT, rhs, start, stop, r):
        op("P", P.matmul, r, [("ps", b)], [b], out=ps[b][:, c0:c1], lhsT=lhsT, rhs=rhs, start=start, stop=stop)

    def fill(ap, val, w):
        op("V", V.memset, [], [w], ap=ap, constant=val)

    def sel(n, pattern, cmp, val, base, mul):
        op("G", g.affine_select, [n], [n], out=T[n][:], in_=T[n][:], pattern=pattern, compare_op=cmp, fill=val, base=base,
           channel_multiplier=mul)

    def iota(n, lo, hi, pattern, base, mul):
        kw = {} if n == "qi" else {"allow_small_or_imprecise_dtypes": True}
        op("G", g.iota, [], [n], out=T[n][:, lo:hi], pattern=pattern, base=base, channel_multiplier=mul, **kw)

    tab, mz, yy, ab, ff, fr, xh = T["tab"], T["mz"], T["yy"], T["ab"], T["ff"], T["fr"], T["xh"]
    msk = [T["mska"], T["mskb"]]
    ps = [T["ps%d" % b] for b in range(8)]
    ident, nident, idpow = T["ident"], T["nident"], T["idpow"]
    zin = [T["zin%d" % t] for t in range(STEPS)]
    nz = [T["nz%d" % t] for t in range(STEPS)]
    mtags = [[("m", s, k) for k in range(9)] for s in range(2)]

    def cols(b):
        return slice(512 * b, 512 * b + 512)

    def mb(t, b):
        return mtags[t % 2][2 * b:2 * b + 2]

    dma("S", g.scalar.dma_start, "ldx", 16, [], ["tab"], out=tab[:, 0:NW], in_=T["xr"][:])
    dma("Y", g.sync.dma_start, "ldz", 16, [], ["z0"], out=zin[0][:], in_=T["z0"][:])
    dma("Y", g.sync.dma_start, "ldm", 16, [], ["mini"], out=T["mini"][:], in_=T["m0"][:])
    dma("Y", g.sync.dma_start, "ldw", 16, [], ["wts"], out=T["wts"][:], in_=T["wt"][:])

    fill(T["sel"][:], 1.0, "sel")
    fill(ident[:], 1.0, "ident")
    fill(T["triw"][:], 1.0, "triw")
    fill(T["ones"][:], 1.0, "ones")
    fill(T["shf"][:], 0.0, "shf")
    fill(msk[0][:, 2048:2304], 0.0, ("m", 0, 8))
    fill(T["lim"][:], 1.5, "lim")
    sel("sel", [[-16, 9], [-1000, 16]], A.is_ge, 0.0, 16, 1)
    sel("sel", [[16, 9], [-1000, 16]], A.is_ge, 0.0, -1, -1)
    sel("ident", [[1, 128]], A.is_equal, 0.0, 0, -1)
    iota("k4", 0, 128, [[4096, 8], [0, 16]], 0, 0)
    sel("triw", [[-16, 8], [0, 16]], A.is_ge, 0.0, 0, 1)
    sel("triw", [[1, 128]], A.is_ge, 0.0, -1, -1)
    sel("triw", [[1, 128]], A.not_equal, -1.0, 0, -1)
    iota("qi", 0, 8, [[0, 8]], 0, 1)
    iota("baseoff", 0, 112, [[256, 7], [16, 16]], 256, 0)
    iota("baseoff", 112, 128, [[16, 16]], 0, 0)
    iota("cmpt", 0, 240, [[1, 15], [0, 16]], 1, 0)
    sel("shf", [[0, 15], [1, 128]], A.not_equal, -1.0, 0, -1)
    sel("shf", [[-1, 15], [1, 128]], A.not_equal, 1.0, -1, -1)

    for k in range(NK):
        ts(mz[:, 256 * k:256 * k + 256], zin[0][:], T["mini"][:, k:k + 1], A.mult, ["z0", "mini"], [("mz", k // 2)])
        if k == 3:
            ts(T["bigu"][:], T["sel"][:], T["wts"][:, 0:1], A.mult, ["sel", "wts"], ["bigu"])
            ts(T["bigv"][:], T["sel"][:], T["wts"][:, 1:2], A.mult, ["sel", "wts"], ["bigv"])

    def constants_first():
        ts(nident[:], ident[:], -1.0, A.mult, ["ident"], ["nident"])
        ts(T["idm512"][:], ident[:], -512.0, A.mult, ["ident"], ["idm512"])
        ts(T["id600"][:], ident[:], 600.0, A.mult, ["ident"], ["id600"])
        for k in range(NK):
            act(msk[0][:, 256 * k:256 * k + 256], msk[0][:, 2048:2304], FN.Identity, [("m", 0, 8), "mini"], [("m", 0, k)],
                bias=T["mini"][:, k:k + 1])

    def constants_mid():
        fill(msk[1][:, 2048:2304], 0.0, ("m", 1, 8))
        fill(T["sgn"][:, 0:1], -1.0, "sgn")
        fill(T["sgn"][:, 1:16], 1.0, "sgn")
        fill(T["ctab"][:, 0:1], 1.0, "ctab")
        fill(T["ctab"][:, 1:8], 0.5 - 1.0 / 4096, "ctab")
        for j in range(8):
            fill(T["thrt"][:, j:j + 1], float(2 ** (8 - j)), "thrt")
        fill(T["thrt"][:, 8:16], 1.0, "thrt")
        fill(T["m256"][:], -256.0, "m256")
        for k in range(NK):
            ts(idpow[:, 128 * k:128 * k + 128], ident[:], float(2 ** (7 - k)), A.mult, ["ident"], ["idpow"])
        ts(T["ident256"][:], ident[:], 256.0, A.mult, ["ident"], ["ident256"])

    def constants_last():
        ts(T["qi"][:], T["qi"][:], 15, A.bitwise_and, ["qi"], ["qi"])
        cp(T["qf"][:], T["qi"][:], ["qi"], ["qf"])
        ts(T["dum"][:], T["qf"][:], float(NW), A.add, ["qf"], ["dum"])
        ts(T["baseoff"][:], T["baseoff"][:], T["qf"][:, 0:1], A.add, ["qf", "baseoff"], ["baseoff"])
        ts(T["cmpt"][:], T["cmpt"][:], T["qf"][:, 0:1], A.is_gt, ["qf", "cmpt"], ["cmpt"], s2=99999.0, o2=A.mult)
        cp(T["shh"][:], T["shf"][:], ["shf"], ["shh"])

    def header(t):
        for h in range(2):
            mm(6, 256 * h, 256 * h + 256, ident[:], zin[t][:], True, True, ["ident", "z%d" % t])
        if t > 0:
            for b in MZV:
                tt(mz[:, cols(b)], msk[t % 2][:, cols(b)], ps[6][:], A.mult, mb(t, b) + [("ps", 6)], [("mz", b)], [6])

    def masked(t):
        for b in MZS:
            mm(b, 0, 512, T["ident256"][:], msk[t % 2][:, cols(b)], True, False, ["ident256"] + mb(t, b))
        for b in MZS:
            for h in range(2):
                mm(b, 256 * h, 256 * h + 256, ident[:], zin[t][:], False, h == 1, ["ident", "z%d" % t])
        for b in MZS:
            act(mz[:, cols(b)], ps[b][:], FN.Relu, [("ps", b), "m256"], [("mz", b)], [b], bias=T["m256"][:, 0:1])

    def tolist(bank, c0, n, src, lo, hi, wt, rtags):
        for q in range(16):
            mm(bank, c0, c0 + n, T[wt][:, 16 - q:144 - q], src[:, lo + q:hi:16], q == 0, q == 15, [wt] + rtags)

    def hashing(x, bank, n):
        a, b, c = "hi%d" % x, "ha%d" % x, "hb%d" % x
        hi, ha, hb = T[a], T[b], T[c]
        return [lambda: cp(hi[:], ps[bank][:, 0:2 * n], [("ps", bank)], [a], [bank]),
                lambda: ts(hi[:], hi[:], 4095, A.bitwise_and, [a], [a]),
                lambda: tt(ha[:], hi[:, 0:n], hi[:, n:2 * n], A.mult, [a], [b]),
                lambda: ts(hb[:], hi[:, 0:n], 37.0, A.mult, [a], [c]),
                lambda: ts(ha[:], ha[:], 5, A.arith_shift_right, [b], [b]),
                lambda: tt(ha[:], ha[:], hb[:], A.add, [b, c], [b])]

    def places(h):
        ha, tag, hu = T["ha%d" % h], "ha%d" % h, "hu%d" % h
        return hashing(h, 4 + h, 64) + [lambda: ts(ha[:], ha[:], 4095, A.bitwise_and, [tag], [tag]),
                                        lambda: cp(T[hu][:], ha[:], [tag], [hu])]

    def limits(t, b):
        mm(SB[b], 0, 512, T["idm512"][:], msk[t % 2][:, cols(b)], True, False, ["idm512"] + mb(t, b))
        mm(SB[b], 0, 512, T["id600"][:], T["ones"][:], False, True, ["id600", "ones"])

    def merge(first, second):
        n = max(len(first), len(second))
        for i in range(n):
            for chain in (first, second):
                for f in chain[i * len(chain) // n:(i + 1) * len(chain) // n]:
                    f()

    def front(t, scatters):
        for h in range(2):
            rt = [("mz", 2 * h), ("mz", 2 * h + 1)]
            tolist(4 + h, 0, 64, mz, 1024 * h, 1024 * h + 1024, "bigu", rt)
            tolist(4 + h, 64, 64, mz, 1024 * h, 1024 * h + 1024, "bigv", rt)
        if t == 0:
            header(0)
            constants_first()
        for b in range(4):
            if b not in SB:
                mm(b, 0, 512, nident[:], mz[:, cols(b)], True, False, ["nident", ("mz", b)])
        limits(t, 0)
        merge([], scatters[:NSC])
        merge(places(0) + places(1), scatters[NSC:])
        if t == 0:
            constants_mid()
        limits(t, 2)

    def gathermask(t, b):
        h, o = b // 2, 32 * (b % 2)
        hu = "hu%d" % h
        win = tab[:, 0:NW].indirect(T[hu][:, o:o + 32])
        if b in SB:
            act(xh[:, cols(b)], win, FN.Copy, ["tab", hu], [("xh", b)])
        else:
            tt(yy[:, cols(b)], win, msk[t % 2][:, cols(b)], A.mult, ["tab", hu] + mb(t, b), [("yy", b)])

    def difference(t, b):
        if b in SB:
            mm(b, 0, 512, ident[:], xh[:, cols(b)], True, False, ["ident", ("xh", b)])
            for h in range(2):
                mm(b, 256 * h, 256 * h + 256, nident[:], zin[t][:], False, h == 1, ["nident", "z%d" % t])
        else:
            mm(b, 0, 512, ident[:], yy[:, cols(b)], False, True, ["ident", ("yy", b)])

    def absol(b):
        act(ab[:, cols(b)], ps[b][:], FN.Abs, [("ps", b)], [("ab", b)], [b])

    def failing(b):
        if b in SB:
            tt(ff[:, cols(b)], ab[:, cols(b)], ps[SB[b]][:], A.is_gt, [("ab", b), ("ps", SB[b])], [("ff", b)], [SB[b]])
        else:
            ts(ff[:, cols(b)], ab[:, cols(b)], float(LIMIT), A.is_gt, [("ab", b)], [("ff", b)])

    def prefix(b):
        mm(b, 0, 512, T["triw"][:], ff[:, cols(b)], True, True, ["triw", ("ff", b)])

    def firsts(b):
        act(fr[:, cols(b)], ps[b][:], FN.Relu, [("ps", b)], [("fr", b)], [b], scale=-1.0)

    def counts(h):
        tolist(4 + h, 0, 64, ff, 1024 * h, 1024 * h + 1024, "sel", [("ff", 2 * h), ("ff", 2 * h + 1)])

    def bases(h):
        x = str(h)
        tt(T["bs" + x][:], T["ha" + x][:], T["k4"][:, 64 * h:64 * h + 64], A.add, ["ha" + x, "k4"], ["bs" + x])

    def keys(h):
        x = str(h)
        ts(T["nk" + x][:], ps[4 + h][:, 0:64], T["lim"][:, 0:1], A.is_gt, [("ps", 4 + h), "lim"], ["nk" + x], [4 + h],
           s2=32768.0, o2=A.mult)
        tt(T["ky" + x][:], T["nk" + x][:], T["bs" + x][:], A.add, ["nk" + x, "bs" + x], ["ky" + x])
        tt(T["ka" + x][:], T["ky" + x][:, 0:32], T["ky" + x][:, 32:64], A.min, ["ky" + x], ["ka" + x])
        tt(T["kb" + x][:], T["ka" + x][:, 0:16], T["ka" + x][:, 16:32], A.min, ["ka" + x], ["kb" + x])

    def moves(ks):
        for k in ks:
            if k == NK:
                ts(T["ob"][:, 112:128], T["jr"][:], 8.0, A.min, ["jr"], ["ob"], s2=256.0, o2=A.mult)
            else:
                ts(T["ob"][:, 16 * k - 16:16 * k], T["jr"][:], float(k), A.is_ge, ["jr"], ["ob"], s2=-256.0, o2=A.mult)

    def scatter(t, c):
        return lambda: cp(tab[:].indirect(T["scu"][:, 2 * c:2 * c + 1]), zin[t][:, 16 * c:16 * c + 16], ["scu", "z%d" % t], ["tab"])

    front(0, [])
    for t in range(STEPS):
        zt, s2 = "z%d" % t, (t + 1) % 2
        cur, nxt, ctags, ntags = msk[t % 2], msk[s2], mtags[t % 2], mtags[s2]
        last = t == STEPS - 1
        for b in range(4):
            gathermask(t, b)
        if t == 0:
            constants_last()
        for b in range(4):
            difference(t, b)
            absol(b)
        failing(0)
        prefix(0)
        failing(1)
        counts(0)
        bases(0)
        bases(1)
        prefix(1)
        failing(2)
        prefix(2)
        failing(3)
        counts(1)
        prefix(3)
        firsts(0)
        firsts(1)
        firsts(2)
        keys(0)
        keys(1)
        tt(T["key"][:], T["kb0"][:], T["kb1"][:], A.min, ["kb0", "kb1"], ["key"])
        ts(T["nmu"][:], T["key"][:], 32768.0, A.is_ge, ["key"], ["nmu"])
        ts(T["hs"][:], T["key"][:], 4095, A.bitwise_and, ["key"], ["hs"])
        tt(T["sz"][:], T["sgn"][:].indirect(T["nmu"][:]), zin[t][:], A.mult, ["sgn", "nmu", zt], ["sz"])
        cp(T["hsu"][:], T["hs"][:], ["hs"], ["hsu"])
        act(T["cc"][:], T["ctab"][:].indirect(T["nmu"][:]), FN.Copy, ["ctab", "nmu"], ["cc"])
        tt(T["yh"][:], tab[:, 0:NW].indirect(T["hsu"][:]), T["sz"][:], A.add, ["tab", "hsu", "sz"], ["yh"])
        firsts(3)
        act(ps[7][:, 0:256], T["yh"][:], FN.Abs, ["yh"], [("ps", 7)], [7])
        ts(T["jr"][:], T["key"][:], 12, A.arith_shift_right, ["key"], ["jr"])
        if not last:
            ts(T["nmf"][:], T["key"][:], 32768.0, A.is_ge, ["key"], ["nmf"])
        cp(T["jru"][:], T["jr"][:], ["jr"], ["jru"])
        act(T["thr"][:], T["thrt"][:].indirect(T["jru"][:]), FN.Copy, ["thrt", "jru"], ["thr"])
        moves(range(1, 1 + NOB))
        tt(T["wh"][:], T["cc"][:], ps[7][:, 0:256], A.mult, ["cc", ("ps", 7)], ["wh"], [7])
        ts(nz[t][:], T["wh"][:], MAGIC, A.add, ["wh"], [("nz", t)], s2=-MAGIC, o2=A.add)
        if not last:
            rid, pid = topo.addr(nxt_core, core)
            hold("G", [("nz", t)], [], ())
            g.remote_dma(out_ap=zin[t + 1][:], in_ap=nz[t][:], remote_sem=T.sem["arr%d" % (t + 1)], local_sem=T.sem["sent"],
                         pid=pid, routing_id=rid, dma_engine_mask=topo.mask(core, nxt_core))
            lastw["z%d" % (t + 1)] = ("arr%d" % (t + 1), len(topo.engines(prv_core, core)))
        dma("Y", g.sync.dma_start, "outs", 16 * (t + 1), [("nz", t)], [], out=T["yz"][:, NP * t:NP * t + NP], in_=nz[t][:])
        moves(range(1 + NOB, 9))
        tt(T["of"][:], T["ob"][:], T["baseoff"][:], A.add, ["ob", "baseoff"], ["of"])
        if not last:
            mm(4, 256, 272, T["ones"][:, 0:128], T["nmf"][:], True, True, ["ones", "nmf"])
        for k in range(NK):
            mm(4, 0, 256, idpow[:, 128 * k:128 * k + 128], fr[:, 256 * k:256 * k + 256], k == 0, k == NK - 1,
               ["idpow", ("fr", k // 2)])
        tt(T["u1"][:], T["thr"][:], ps[4][:, 0:256], A.is_le, ["thr", ("ps", 4)], ["u1"], [4])
        cp(T["offu"][:], T["of"][:], ["of"], ["offu"])
        low = cur[:].indirect(T["offu"][:, 0:48])
        if not last:
            act(nxt[:, 256:1024], low, FN.Copy, ctags + ["offu"], ntags[1:4])
        act(nxt[:, 1024:2048], cur[:].indirect(T["offu"][:, 48:112]), FN.Copy, ctags + ["offu"], ntags[4:8])
        tt(nxt[:, 0:256], cur[:].indirect(T["offu"][:, 112:128]), T["u1"][:], A.max, ctags + ["offu", "u1"], [ntags[0]])
        if last:
            cp(nxt[:, 256:1024], low, ctags + ["offu"], ntags[1:4])
            break
        tt(T["uz"][:], nxt[:, 0:256], ps[6][:, 0:256], A.mult, [ntags[0], ("ps", 6)], ["uz"], [6])
        tolist(5, 0, 16, T["uz"], 0, 256, "bigu", ["uz"])
        tolist(5, 16, 16, T["uz"], 0, 256, "bigv", ["uz"])
        op("V", V.tensor_reduce, [("ps", 4)], ["asum"], [4], out=T["asum"][:], in_=ps[4][:, 256:272], axis=AxisListType.X, op=A.add)
        cp(T["ai"][:, 0:1], T["asum"][:], ["asum"], ["ai"])
        ts(T["ai"][:, 0:1], T["ai"][:, 0:1], 1, A.bitwise_and, ["ai"], ["ai"])
        ts(T["lim"][:, 0:1], T["ai"][:, 0:1], 1.5, A.add, ["ai"], ["lim"])
        for f in hashing(2, 5, 16):
            f()
        ts(T["pl"][:], T["ha2"][:], 4095, A.bitwise_and, ["ha2"], ["pl"])
        ts(T["hlb"][:], T["pl"][:], -2048.0, A.add, ["pl"], ["hlb"])
        header(t + 1)
        for d in range(15):
            mm(7, 16 * d, 16 * d + 16, T["shh"][:, 128 * d:128 * d + 128], T["hlb"][:], True, True, ["shh", "hlb"])
        masked(t + 1)
        tt(T["eq"][:], T["cmpt"][:], ps[7][:, 0:240], A.is_equal, ["cmpt", ("ps", 7)], ["eq"], [7])
        for d in range(15):
            mm(5, 32, 48, ident[:], T["eq"][:, 16 * d:16 * d + 16], d == 0, d == 14, ["ident", "eq"])
        ts(T["lo"][:], ps[5][:, 32:48], 0.5, A.is_gt, [("ps", 5), "dum"], ["lo"], [5], s2=T["dum"][:, 0:1], o2=A.mult)
        tt(T["so"][:], T["lo"][:], T["pl"][:], A.max, ["lo", "pl"], ["so"])
        cp(T["scu"][:, 0:32:2], T["so"][:], ["so"], ["scu"])
        front(t + 1, [scatter(t, c) for c in range(15, -1, -1)])
    s2 = STEPS % 2
    n = 16 * STEPS
    for lo, hi, tags in ((0, 256, mtags[s2][0:1]), (256, 1024, mtags[s2][1:4]), (1024, 2048, mtags[s2][4:8])):
        n += 16
        dma("Y", g.sync.dma_start, "outs", n, tags, [], out=T["ym"][:, lo:hi], in_=msk[s2][:, lo:hi])
    g.sync.wait_ge(T.sem["outs"], n)
    for e in ("V", "S", "P", "G"):
        g.sync.wait_ge(T.sem[semof[e]], count[e])
    g.wait_ge(T.sem["sent"], (STEPS - 1) * len(topo.engines(core, nxt_core)))
